import numpy as np
import ml_dtypes


def mxq(x, axis, fmt="e4m3"):
    dtype, down = {"e4m3": (ml_dtypes.float8_e4m3fn, 7), "e5m2": (ml_dtypes.float8_e5m2, 14)}[fmt]
    v = np.moveaxis(np.asarray(x, np.float32).astype(ml_dtypes.bfloat16).astype(np.float64), axis, -1)
    blocks = v.reshape(v.shape[:-1] + (-1, 32))
    amax = np.abs(blocks).max(-1, keepdims=True)
    byte = np.maximum(np.where(amax > 0, np.frexp(amax)[1] - 1 + 127, 0) - down, 1)
    scale = np.exp2(byte - 127.0)
    codes = (blocks / scale).astype(np.float32).astype(dtype).astype(np.float64)
    return np.moveaxis((codes * scale).reshape(v.shape), -1, axis)


WIDE = False


def mx_kscale(k):
    if not WIDE:
        return np.ones(k)
    levels = np.array([30, -30])
    if k % 512:
        return np.exp2(np.random.permutation(np.resize(levels, k // 32))).repeat(32)
    a = np.empty((k // 512, 16))
    for p in range(k // 512):
        a[p, :8] = np.random.permutation(np.resize(levels, 8))
        for g in range(8):
            far = levels[np.abs(levels - a[p, g]) >= 10]
            a[p, g + 8] = far[np.random.randint(len(far))]
    return np.exp2(a.ravel()).repeat(32)


def f64(x):
    return np.asarray(x).astype(np.float64)


def striped(idx):
    return np.tile(np.asarray(idx).reshape(-1, 16).T, (8, 1)).astype(np.uint16)


def unstriped(offs):
    return offs[:16].T.reshape(-1).astype(np.int64)


E2M1 = np.array([0.0, 0.5, 1.0, 1.5, 2.0, 3.0, 4.0, 6.0, -0.0, -0.5, -1.0, -1.5, -2.0, -3.0, -4.0, -6.0])


def pack_weight(w, fmt):
    k, n = w.shape
    w = f64(np.asarray(w, np.float32).astype(ml_dtypes.bfloat16)).reshape(k // 32, 32, n)
    amax = np.abs(w).max(1)
    if fmt == "e4m3":
        byte = np.frexp(amax)[1] - 1 + 127 - 7
    else:
        mant, ex = np.frexp(amax / 6.0)
        byte = np.where(mant > 0.5, ex, ex - 1) + 127
    byte = np.clip(np.where(amax > 0, byte, 1), 1, 254)
    scaled = (w * np.exp2(127.0 - byte)[:, None, :]).reshape(k, n).astype(np.float32)
    by_word = np.ascontiguousarray(scaled.reshape(k // 512, 128, 4, n).transpose(0, 1, 3, 2))
    if fmt == "e4m3":
        words = by_word.astype(ml_dtypes.float8_e4m3fn).view(np.uint8)
    else:
        c = by_word.astype(ml_dtypes.float4_e2m1fn).view(np.uint8) & 0xF
        words = (c[..., 0::2] | (c[..., 1::2] << 4)).reshape(k // 512, 128, 2 * n)
    return np.ascontiguousarray(words), np.ascontiguousarray(byte.astype(np.uint8).reshape(k // 512, 16, n))


def unpack_weight(words, scales, fmt):
    g, _, n = scales.shape
    words = np.ascontiguousarray(words).reshape(g, 128, n, -1)
    if fmt == "e4m3":
        vals = words.view(ml_dtypes.float8_e4m3fn).astype(np.float64)
    else:
        nib = np.empty((g, 128, n, 4), np.uint8)
        nib[..., 0::2] = words & 0xF
        nib[..., 1::2] = words >> 4
        vals = E2M1[nib]
    vals = vals * np.repeat(np.exp2(scales.astype(np.float64) - 127.0), 8, axis=1)[..., None]
    return vals.transpose(0, 1, 3, 2).reshape(g * 512, n)


K, J, N, R, T, V = 512, 512, 256, 256, 1024, 1024


def setup_inputs():
    n = np.random.standard_normal
    idx = np.random.permutation(T)[:J]
    idx2 = np.random.permutation(V)[:J]
    fj = mx_kscale(J)
    fk = mx_kscale(K)
    drp = pack_weight(n((K, R)) * 1 / np.sqrt(K) / fk[:, None], "e2m1")
    return {
        "xf": (n((K, T))).astype(np.float32),
        "ra": (np.random.uniform(0.5, 1.5, (1, J)) * fj).astype(np.float32),
        "lo": (np.random.uniform(-0.3, 0.5, (K, 1))).astype(np.float32),
        "gt": (n((N, V)) * np.exp(0.5 * n((1, V)))).astype(np.float32),
        "rb": (np.random.uniform(0.5, 1.5, (1, J)) / fj).astype(np.float32),
        "sv": (n((N, V))).astype(np.float32),
        "fkr": (np.random.uniform(0.5, 1.5, (1, K)) * fk).astype(np.float32),
        "dr_words": drp[0],
        "dr_scales": drp[1],
        "old": (12.0 * n((R, N))).astype(np.float32),
        "offs": striped(idx),
        "offs2": striped(idx2),
    }


def reference(xf, ra, lo, gt, rb, sv, fkr, dr_words, dr_scales, old, offs, offs2):
    idx = unstriped(offs)
    idx2 = unstriped(offs2)
    dru = unpack_weight(dr_words, dr_scales, "e2m1")
    us = np.maximum(f64(xf)[:, idx] - f64(lo), 0.0) * f64(ra)
    ut = us.T
    uj = ut * f64(fkr)
    gs = f64(gt)[:, idx2] * np.maximum(f64(sv)[:, idx2], 0.0) * f64(rb)
    gj = gs.T
    ujq = mxq(uj, 0, "e4m3")
    gjq = mxq(gj, 0, "e5m2")
    w = ujq.T @ gjq
    wq = mxq(w, 0, "e5m2")
    v2 = dru.T @ wq
    y = 0.05 * np.maximum(v2, f64(old))
    return y

@@ -1,0 +1,182 @@
+from contextlib import ExitStack
+
+import concourse.mybir as mybir
+from concourse.masks import make_identity
+
+K, J, N, R, T = 512, 512, 256, 256, 1024
+FLOPS = 2 * J * K * N + 2 * K * R * N
+
+F32 = mybir.dt.float32
+BF16 = mybir.dt.bfloat16
+U32 = mybir.dt.uint32
+I32 = mybir.dt.int32
+U16 = mybir.dt.uint16
+U8 = mybir.dt.uint8
+E4M3 = mybir.dt.float8_e4m3fn_x4
+E5M2 = mybir.dt.float8_e5m2_x4
+E2M1 = mybir.dt.float4_e2m1fn_x4
+ALU = mybir.AluOpType
+COPY = mybir.ActivationFunctionType.Copy
+
+P = 128
+PACK = 4
+
+
+def tile_list_directions_over_saved_larger_kernel(
+    tc, xf, ra, lo, gt, rb, sv, fkr, dr_words, dr_scales, old, offs, offs2, out
+):
+    nc = tc.nc
+    with ExitStack() as ctx:
+        keep = ctx.enter_context(tc.tile_pool(name="keep", bufs=1))
+        psum = ctx.enter_context(tc.psum_pool(name="psum", bufs=1))
+
+        def sbuf(name, shape, dtype):
+            return keep.tile(shape, dtype, name=name, align_bytes=64)
+
+        x_rows = xf.rearrange("(p t) v -> p t v", t=PACK)
+        x_win = [sbuf("x_win%d" % t, [P, T], F32) for t in range(PACK)]
+        g_win = [sbuf("g_win%d" % h, [P, T], F32) for h in range(2)]
+        s_win = [sbuf("s_win%d" % h, [P, T], F32) for h in range(2)]
+        list1 = keep.tile([P, J // 16], U16, name="list1")
+        list2 = keep.tile([P, J // 16], U16, name="list2")
+        ra4 = sbuf("ra4", [P, PACK], F32)
+        rb4 = sbuf("rb4", [P, PACK], F32)
+        lo4 = sbuf("lo4", [P, PACK], F32)
+        fk4 = sbuf("fk4", [P, PACK], F32)
+        old_sb = sbuf("old_sb", [P, 2, N], F32)
+        dr_w = sbuf("dr_w", [P, 2 * R], U8)
+        dr_s = sbuf("dr_s", [P, R], U8)
+        ident = sbuf("ident", [P, P], F32)
+
+        nc.sync.dma_start(x_win[0][:], x_rows[:, 0, :])
+        nc.sync.dma_start(list1[:], offs)
+        nc.scalar.dma_start(ra4[:], ra.rearrange("o (p t) -> (o p) t", t=PACK))
+        nc.scalar.dma_start(lo4[:], lo.rearrange("(p t) o -> p (t o)", t=PACK))
+        nc.scalar.dma_start(fk4[:], fkr.rearrange("o (p t) -> (o p) t", t=PACK))
+        nc.scalar.dma_start(rb4[:], rb.rearrange("o (p t) -> (o p) t", t=PACK))
+        for t in range(1, PACK):
+            nc.sync.dma_start(x_win[t][:], x_rows[:, t, :])
+        nc.sync.dma_start(list2[:], offs2)
+        for h in range(2):
+            nc.sync.dma_start(g_win[h][:], gt[h * P : (h + 1) * P, :])
+            nc.sync.dma_start(s_win[h][:], sv[h * P : (h + 1) * P, :])
+        nc.sync.dma_start(dr_w[:].bitcast(I32), dr_words[0].bitcast(I32))
+        nc.sync.dma_start(old_sb[:], old.rearrange("(h p) n -> p h n", p=P))
+
+        make_identity(nc, ident[:])
+        nc.gpsimd.memset(dr_s[:].bitcast(I32), 0)
+        for q in range(4):
+            nc.sync.dma_start(
+                dr_s[32 * q : 32 * q + 4, :].bitcast(I32), dr_scales[0, 4 * q : 4 * q + 4, :].bitcast(I32)
+            )
+
+        def spread(name, col4):
+            bank = psum.tile([P, PACK, P], F32, name=name)
+            for t in range(PACK):
+                nc.tensor.transpose(bank[:, t, :], col4[:, t : t + 1].to_broadcast([P, P]), ident[:])
+            return bank[:].rearrange("p t q -> p q t")
+
+        ra_all = spread("ra_bank", ra4)
+        rb_bank = spread("rb_bank", rb4)
+        rb_all = sbuf("rb_all", [P, J], F32)
+
+        def by_four(ap):
+            return ap.rearrange("p (q t) -> p q t", t=PACK)
+
+        def turn(name, rounded, slot, on_scalar):
+            words = rounded[:].bitcast(F32)
+            bank = psum.tile([P, 2, P], F32, name=name + "_bank", tag="turn%d" % slot)
+            for u in range(2):
+                nc.tensor.transpose(bank[:, u, :], words[:, u : 2 * P : 2], ident[:])
+            grouped = sbuf(name + "_grouped", [P, P * PACK], BF16)
+            dst = grouped[:].bitcast(F32).rearrange("p (r u) -> p r u", u=2)
+            src = bank[:].rearrange("p u r -> p r u")
+            if on_scalar:
+                nc.scalar.copy(dst, src)
+            else:
+                nc.vector.tensor_copy(dst, src)
+            return grouped
+
+        def quantise(name, grouped, fmt):
+            codes = sbuf(name + "_codes", [P, P], U32)
+            scales = sbuf(name + "_scales", [P, P], U8)
+            nc.vector.quantize_mx(out=codes[:].bitcast(fmt), scales=scales[:], in_=grouped[:])
+            return codes, scales
+
+        u_mx = []
+        u_rounded = []
+        for t in range(PACK + 1):
+            if t < PACK:
+                picked = sbuf("x_picked%d" % t, [P, J], F32)
+                nc.scalar.activation(picked[:], x_win[t][:].indirect(list1[:]), COPY)
+                over = sbuf("x_over%d" % t, [P, J], F32)
+                nc.vector.tensor_scalar(over[:], picked[:], lo4[:, t : t + 1], 0.0, ALU.subtract, ALU.max)
+                rounded = sbuf("u_rounded%d" % t, [P, J], BF16)
+                nc.vector.scalar_tensor_tensor(
+                    by_four(rounded[:]), by_four(over[:]), fk4[:, t : t + 1], ra_all, ALU.mult, ALU.mult
+                )
+                u_rounded.append(rounded)
+            if t == 0:
+                nc.vector.tensor_copy(by_four(rb_all[:]), rb_bank)
+            if t > 0:
+                grouped = turn("u%d" % (t - 1), u_rounded[t - 1], t % 2, t % 2 == 0)
+                u_mx.append(quantise("u%d" % (t - 1), grouped, E4M3))
+
+        old_part = sbuf("old_part", [P, 2, N], F32)
+        out_rows = out.rearrange("(h p) n -> p h n", p=P)
+
+        def front(h):
+            g_picked = sbuf("g_picked%d" % h, [P, J], F32)
+            nc.vector.tensor_tensor(g_picked[:], g_win[h][:].indirect(list2[:]), rb_all[:], ALU.mult)
+            s_picked = sbuf("s_picked%d" % h, [P, J], F32)
+            rounded = sbuf("g_rounded%d" % h, [P, J], BF16)
+            half = J // 2
+            nc.vector.tensor_copy(s_picked[:, :half], s_win[h][:].indirect(list2[:, : half // 16]))
+            nc.scalar.activation(s_picked[:, half:], s_win[h][:].indirect(list2[:, half // 16 :]), COPY)
+            for c in range(2):
+                cols = slice(c * half, (c + 1) * half)
+                nc.vector.scalar_tensor_tensor(
+                    rounded[:, cols], s_picked[:, cols], 0.0, g_picked[:, cols], ALU.max, ALU.mult
+                )
+            grouped = turn("g%d" % h, rounded, h, True)
+            return quantise("g%d" % h, grouped, E5M2)
+
+        def back(h, g_mx):
+            g_codes, g_scales = g_mx
+            w_bank = psum.tile([P, PACK, P], F32, name="w_bank%d" % h)
+            for t in range(PACK):
+                u_codes, u_scales = u_mx[t]
+                nc.tensor.matmul_mx(
+                    out=w_bank[:, t, :],
+                    lhsT=u_codes[:].bitcast(E4M3),
+                    lhsT_scale=u_scales[:],
+                    rhs=g_codes[:].bitcast(E5M2),
+                    rhs_scale=g_scales[:],
+                    start=True,
+                    stop=True,
+                )
+            w_grouped = sbuf("w_grouped%d" % h, [P, P * PACK], BF16)
+            nc.scalar.copy(by_four(w_grouped[:]), w_bank[:].rearrange("p t n -> p n t"))
+            w_codes, w_scales = quantise("w%d" % h, w_grouped, E5M2)
+            v_bank = psum.tile([P, 2, P], F32, name="v_bank%d" % h)
+            for r in range(2):
+                nc.tensor.matmul_mx(
+                    out=v_bank[:, r, :],
+                    lhsT=dr_w[:, 2 * P * r : 2 * P * (r + 1)].bitcast(E2M1),
+                    lhsT_scale=dr_s[:, P * r : P * (r + 1)],
+                    rhs=w_codes[:].bitcast(E5M2),
+                    rhs_scale=w_scales[:],
+                    start=True,
+                    stop=True,
+                )
+            result = sbuf("result%d" % h, [P, 2, P], F32)
+            nc.vector.scalar_tensor_tensor(
+                result[:], v_bank[:], 0.05, old_part[:, :, h * P : (h + 1) * P], ALU.mult, ALU.max
+            )
+            nc.sync.dma_start(out_rows[:, :, h * P : (h + 1) * P], result[:])
+
+        g0 = front(0)
+        g1 = front(1)
+        nc.scalar.activation(old_part[:], old_sb[:], COPY, scale=0.05)
+        back(0, g0)
+        back(1, g1)

@@ -30,8 +30,8 @@ def tile_list_directions_over_saved_larger_kernel(
         keep = ctx.enter_context(tc.tile_pool(name="keep", bufs=1))
         psum = ctx.enter_context(tc.psum_pool(name="psum", bufs=1))
 
-        def sbuf(name, shape, dtype):
-            return keep.tile(shape, dtype, name=name, align_bytes=64)
+        def sbuf(name, shape, dtype, tag=""):
+            return keep.tile(shape, dtype, name=name, tag=tag or name, align_bytes=64)
 
         x_rows = xf.rearrange("(p t) v -> p t v", t=PACK)
         x_win = [sbuf("x_win%d" % t, [P, T], F32) for t in range(PACK)]
@@ -50,20 +50,24 @@ def tile_list_directions_over_saved_larger_kernel(
 
         nc.sync.dma_start(x_win[0][:], x_rows[:, 0, :])
         nc.sync.dma_start(list1[:], offs)
-        nc.scalar.dma_start(ra4[:], ra.rearrange("o (p t) -> (o p) t", t=PACK))
-        nc.scalar.dma_start(lo4[:], lo.rearrange("(p t) o -> p (t o)", t=PACK))
-        nc.scalar.dma_start(fk4[:], fkr.rearrange("o (p t) -> (o p) t", t=PACK))
-        nc.scalar.dma_start(rb4[:], rb.rearrange("o (p t) -> (o p) t", t=PACK))
-        for t in range(1, PACK):
+        nc.sync.dma_start(ra4[:], ra.rearrange("o (p t) -> (o p) t", t=PACK))
+        nc.sync.dma_start(lo4[:], lo.rearrange("(p t) o -> p (t o)", t=PACK))
+        nc.sync.dma_start(fk4[:], fkr.rearrange("o (p t) -> (o p) t", t=PACK))
+        nc.sync.dma_start(x_win[1][:], x_rows[:, 1, :])
+        nc.sync.dma_start(rb4[:], rb.rearrange("o (p t) -> (o p) t", t=PACK))
+        for t in range(2, PACK):
             nc.sync.dma_start(x_win[t][:], x_rows[:, t, :])
         nc.sync.dma_start(list2[:], offs2)
         for h in range(2):
             nc.sync.dma_start(g_win[h][:], gt[h * P : (h + 1) * P, :])
+        for h in range(2):
             nc.sync.dma_start(s_win[h][:], sv[h * P : (h + 1) * P, :])
         nc.sync.dma_start(dr_w[:].bitcast(I32), dr_words[0].bitcast(I32))
         nc.sync.dma_start(old_sb[:], old.rearrange("(h p) n -> p h n", p=P))
 
-        make_identity(nc, ident[:])
+        ident_narrow = sbuf("ident_narrow", [P, P], BF16, tag="stage")
+        make_identity(nc, ident_narrow[:])
+        nc.scalar.activation(ident[:], ident_narrow[:], COPY)
         nc.gpsimd.memset(dr_s[:].bitcast(I32), 0)
         for q in range(4):
             nc.sync.dma_start(
@@ -83,73 +87,71 @@ def tile_list_directions_over_saved_larger_kernel(
         def by_four(ap):
             return ap.rearrange("p (q t) -> p q t", t=PACK)
 
-        def turn(name, rounded, slot, on_scalar):
+        def turn(bank, rounded):
             words = rounded[:].bitcast(F32)
-            bank = psum.tile([P, 2, P], F32, name=name + "_bank", tag="turn%d" % slot)
             for u in range(2):
                 nc.tensor.transpose(bank[:, u, :], words[:, u : 2 * P : 2], ident[:])
-            grouped = sbuf(name + "_grouped", [P, P * PACK], BF16)
-            dst = grouped[:].bitcast(F32).rearrange("p (r u) -> p r u", u=2)
-            src = bank[:].rearrange("p u r -> p r u")
-            if on_scalar:
-                nc.scalar.copy(dst, src)
-            else:
-                nc.vector.tensor_copy(dst, src)
-            return grouped
 
-        def quantise(name, grouped, fmt):
-            codes = sbuf(name + "_codes", [P, P], U32)
-            scales = sbuf(name + "_scales", [P, P], U8)
+        def quantise(name, grouped, width, fmt):
+            codes = sbuf(name + "_codes", [P, width], U32)
+            scales = sbuf(name + "_scales", [P, width], U8)
             nc.vector.quantize_mx(out=codes[:].bitcast(fmt), scales=scales[:], in_=grouped[:])
             return codes, scales
 
-        u_mx = []
-        u_rounded = []
-        for t in range(PACK + 1):
-            if t < PACK:
-                picked = sbuf("x_picked%d" % t, [P, J], F32)
-                nc.scalar.activation(picked[:], x_win[t][:].indirect(list1[:]), COPY)
-                over = sbuf("x_over%d" % t, [P, J], F32)
-                nc.vector.tensor_scalar(over[:], picked[:], lo4[:, t : t + 1], 0.0, ALU.subtract, ALU.max)
-                rounded = sbuf("u_rounded%d" % t, [P, J], BF16)
-                nc.vector.scalar_tensor_tensor(
-                    by_four(rounded[:]), by_four(over[:]), fk4[:, t : t + 1], ra_all, ALU.mult, ALU.mult
-                )
-                u_rounded.append(rounded)
+        half = J // 2
+        u_banks = [psum.tile([P, 2, 2, P], F32, name="u_bank%d" % c, tag="u_bank%d" % c) for c in range(2)]
+        x_picked = sbuf("x_picked", [P, PACK, J], F32, tag="stage")
+        for t in range(PACK):
+            picked = x_picked[:, t, :]
+            if t == 0:
+                nc.vector.tensor_copy(picked[:, :half], x_win[t][:].indirect(list1[:, : half // 16]))
+                nc.scalar.activation(picked[:, half:], x_win[t][:].indirect(list1[:, half // 16 :]), COPY)
+            else:
+                nc.scalar.activation(picked, x_win[t][:].indirect(list1[:]), COPY)
+            over = sbuf("x_over%d" % t, [P, J], F32)
+            nc.vector.tensor_scalar(over[:], picked, lo4[:, t : t + 1], 0.0, ALU.subtract, ALU.max)
+            rounded = sbuf("u_rounded%d" % t, [P, J], BF16)
+            nc.vector.scalar_tensor_tensor(
+                by_four(rounded[:]), by_four(over[:]), fk4[:, t : t + 1], ra_all, ALU.mult, ALU.mult
+            )
+            turn(u_banks[t // 2][:, t % 2], rounded)
             if t == 0:
                 nc.vector.tensor_copy(by_four(rb_all[:]), rb_bank)
-            if t > 0:
-                grouped = turn("u%d" % (t - 1), u_rounded[t - 1], t % 2, t % 2 == 0)
-                u_mx.append(quantise("u%d" % (t - 1), grouped, E4M3))
+        u_grouped = sbuf("u_grouped", [P, K * PACK], BF16, tag="stage")
+        u_words = u_grouped[:].bitcast(F32).rearrange("p (c t r u) -> p c t r u", c=2, t=2, u=2)
+        for c in range(2):
+            nc.scalar.copy(u_words[:, c], u_banks[c][:].rearrange("p t u r -> p t r u"))
 
         old_part = sbuf("old_part", [P, 2, N], F32)
         out_rows = out.rearrange("(h p) n -> p h n", p=P)
 
+        g_picked = []
+        for h in range(2):
+            picked = sbuf("g_picked%d" % h, [P, J], F32)
+            nc.vector.tensor_tensor(picked[:], g_win[h][:].indirect(list2[:]), rb_all[:], ALU.mult)
+            g_picked.append(picked)
+
         def front(h):
-            g_picked = sbuf("g_picked%d" % h, [P, J], F32)
-            nc.vector.tensor_tensor(g_picked[:], g_win[h][:].indirect(list2[:]), rb_all[:], ALU.mult)
             s_picked = sbuf("s_picked%d" % h, [P, J], F32)
             rounded = sbuf("g_rounded%d" % h, [P, J], BF16)
-            half = J // 2
-            nc.vector.tensor_copy(s_picked[:, :half], s_win[h][:].indirect(list2[:, : half // 16]))
-            nc.scalar.activation(s_picked[:, half:], s_win[h][:].indirect(list2[:, half // 16 :]), COPY)
-            for c in range(2):
-                cols = slice(c * half, (c + 1) * half)
-                nc.vector.scalar_tensor_tensor(
-                    rounded[:, cols], s_picked[:, cols], 0.0, g_picked[:, cols], ALU.max, ALU.mult
-                )
-            grouped = turn("g%d" % h, rounded, h, True)
-            return quantise("g%d" % h, grouped, E5M2)
+            nc.scalar.activation(s_picked[:], s_win[h][:].indirect(list2[:]), COPY)
+            nc.vector.scalar_tensor_tensor(rounded[:], s_picked[:], 0.0, g_picked[h][:], ALU.max, ALU.mult)
+            bank = psum.tile([P, 2, P], F32, name="g_bank%d" % h)
+            turn(bank, rounded)
+            grouped = sbuf("g_grouped%d" % h, [P, P * PACK], BF16)
+            nc.scalar.copy(
+                grouped[:].bitcast(F32).rearrange("p (r u) -> p r u", u=2), bank[:].rearrange("p u r -> p r u")
+            )
+            return grouped
 
         def back(h, g_mx):
             g_codes, g_scales = g_mx
             w_bank = psum.tile([P, PACK, P], F32, name="w_bank%d" % h)
             for t in range(PACK):
-                u_codes, u_scales = u_mx[t]
                 nc.tensor.matmul_mx(
                     out=w_bank[:, t, :],
-                    lhsT=u_codes[:].bitcast(E4M3),
-                    lhsT_scale=u_scales[:],
+                    lhsT=u_codes[:, t * P : (t + 1) * P].bitcast(E4M3),
+                    lhsT_scale=u_scales[:, t * P : (t + 1) * P],
                     rhs=g_codes[:].bitcast(E5M2),
                     rhs_scale=g_scales[:],
                     start=True,
@@ -157,8 +159,8 @@ def tile_list_directions_over_saved_larger_kernel(
                 )
             w_grouped = sbuf("w_grouped%d" % h, [P, P * PACK], BF16)
             nc.scalar.copy(by_four(w_grouped[:]), w_bank[:].rearrange("p t n -> p n t"))
-            w_codes, w_scales = quantise("w%d" % h, w_grouped, E5M2)
-            v_bank = psum.tile([P, 2, P], F32, name="v_bank%d" % h)
+            w_codes, w_scales = quantise("w%d" % h, w_grouped, P, E5M2)
+            v_bank = psum.tile([P, 2, P], F32, name="v_bank%d" % h, tag="u_bank%d" % h)
             for r in range(2):
                 nc.tensor.matmul_mx(
                     out=v_bank[:, r, :],
@@ -175,8 +177,9 @@ def tile_list_directions_over_saved_larger_kernel(
             )
             nc.sync.dma_start(out_rows[:, :, h * P : (h + 1) * P], result[:])
 
-        g0 = front(0)
-        g1 = front(1)
+        grouped = [front(h) for h in range(2)]
+        u_codes, u_scales = quantise("u", u_grouped, K, E4M3)
+        g_mx = [quantise("g%d" % h, grouped[h], P, E5M2) for h in range(2)]
         nc.scalar.activation(old_part[:], old_sb[:], COPY, scale=0.05)
-        back(0, g0)
-        back(1, g1)
+        for h in range(2):
+            back(h, g_mx[h])

@@ -28,6 +28,8 @@ def tile_list_directions_over_saved_larger_kernel(
     nc = tc.nc
     with ExitStack() as ctx:
         keep = ctx.enter_context(tc.tile_pool(name="keep", bufs=1))
+        stage = ctx.enter_context(tc.tile_pool(name="stage", bufs=1))
+        chain = ctx.enter_context(tc.tile_pool(name="chain", bufs=1))
         psum = ctx.enter_context(tc.psum_pool(name="psum", bufs=1))
 
         def sbuf(name, shape, dtype, tag=""):
@@ -59,30 +61,32 @@ def tile_list_directions_over_saved_larger_kernel(
             nc.sync.dma_start(x_win[t][:], x_rows[:, t, :])
         nc.sync.dma_start(list2[:], offs2)
         for h in range(2):
-            nc.sync.dma_start(g_win[h][:], gt[h * P : (h + 1) * P, :])
-        for h in range(2):
             nc.sync.dma_start(s_win[h][:], sv[h * P : (h + 1) * P, :])
+        for h in range(2):
+            nc.sync.dma_start(g_win[h][:], gt[h * P : (h + 1) * P, :])
         nc.sync.dma_start(dr_w[:].bitcast(I32), dr_words[0].bitcast(I32))
         nc.sync.dma_start(old_sb[:], old.rearrange("(h p) n -> p h n", p=P))
 
-        ident_narrow = sbuf("ident_narrow", [P, P], BF16, tag="stage")
-        make_identity(nc, ident_narrow[:])
-        nc.scalar.activation(ident[:], ident_narrow[:], COPY)
+        ident_narrow = stage.tile([P, 5 * 2 * J], BF16, name="ident_narrow", offset=0)
+        make_identity(nc, ident_narrow[:, :P])
+        nc.scalar.activation(ident[:], ident_narrow[:, :P], COPY)
         nc.gpsimd.memset(dr_s[:].bitcast(I32), 0)
         for q in range(4):
             nc.sync.dma_start(
                 dr_s[32 * q : 32 * q + 4, :].bitcast(I32), dr_scales[0, 4 * q : 4 * q + 4, :].bitcast(I32)
             )
 
+        def placed(name, shape, dtype, half_kib):
+            return chain.tile(shape, dtype, name=name, offset=512 * half_kib, align_bytes=64)
+
         def spread(name, col4):
-            bank = psum.tile([P, PACK, P], F32, name=name)
+            bank = psum.tile([P, PACK, P], F32, name=name, tag=name)
             for t in range(PACK):
                 nc.tensor.transpose(bank[:, t, :], col4[:, t : t + 1].to_broadcast([P, P]), ident[:])
             return bank[:].rearrange("p t q -> p q t")
 
         ra_all = spread("ra_bank", ra4)
-        rb_bank = spread("rb_bank", rb4)
-        rb_all = sbuf("rb_all", [P, J], F32)
+        rb_all = spread("rb_bank", rb4)
 
         def by_four(ap):
             return ap.rearrange("p (q t) -> p q t", t=PACK)
@@ -92,94 +96,119 @@ def tile_list_directions_over_saved_larger_kernel(
             for u in range(2):
                 nc.tensor.transpose(bank[:, u, :], words[:, u : 2 * P : 2], ident[:])
 
-        def quantise(name, grouped, width, fmt):
-            codes = sbuf(name + "_codes", [P, width], U32)
-            scales = sbuf(name + "_scales", [P, width], U8)
+        def quantise(name, grouped, codes, fmt):
+            scales = sbuf(name + "_scales", list(codes.shape), U8)
             nc.vector.quantize_mx(out=codes[:].bitcast(fmt), scales=scales[:], in_=grouped[:])
             return codes, scales
 
         half = J // 2
+        seen = {}
         u_banks = [psum.tile([P, 2, 2, P], F32, name="u_bank%d" % c, tag="u_bank%d" % c) for c in range(2)]
-        x_picked = sbuf("x_picked", [P, PACK, J], F32, tag="stage")
         for t in range(PACK):
-            picked = x_picked[:, t, :]
+            picked = stage.tile([P, J], F32, name="x_picked%d" % t, offset=(0, 2048, 4096, 7168)[t])
             if t == 0:
                 nc.vector.tensor_copy(picked[:, :half], x_win[t][:].indirect(list1[:, : half // 16]))
                 nc.scalar.activation(picked[:, half:], x_win[t][:].indirect(list1[:, half // 16 :]), COPY)
             else:
-                nc.scalar.activation(picked, x_win[t][:].indirect(list1[:]), COPY)
-            over = sbuf("x_over%d" % t, [P, J], F32)
-            nc.vector.tensor_scalar(over[:], picked, lo4[:, t : t + 1], 0.0, ALU.subtract, ALU.max)
+                nc.scalar.activation(picked[:], x_win[t][:].indirect(list1[:]), COPY)
+            over = placed("x_over%d" % t, [P, J], F32, 2 * t)
+            nc.vector.tensor_scalar(over[:], picked[:], lo4[:, t : t + 1], 0.0, ALU.subtract, ALU.max)
             rounded = sbuf("u_rounded%d" % t, [P, J], BF16)
             nc.vector.scalar_tensor_tensor(
                 by_four(rounded[:]), by_four(over[:]), fk4[:, t : t + 1], ra_all, ALU.mult, ALU.mult
             )
             turn(u_banks[t // 2][:, t % 2], rounded)
-            if t == 0:
-                nc.vector.tensor_copy(by_four(rb_all[:]), rb_bank)
-        u_grouped = sbuf("u_grouped", [P, K * PACK], BF16, tag="stage")
-        u_words = u_grouped[:].bitcast(F32).rearrange("p (c t r u) -> p c t r u", c=2, t=2, u=2)
-        for c in range(2):
-            nc.scalar.copy(u_words[:, c], u_banks[c][:].rearrange("p t u r -> p t r u"))
 
-        old_part = sbuf("old_part", [P, 2, N], F32)
-        out_rows = out.rearrange("(h p) n -> p h n", p=P)
-
-        g_picked = []
-        for h in range(2):
-            picked = sbuf("g_picked%d" % h, [P, J], F32)
-            nc.vector.tensor_tensor(picked[:], g_win[h][:].indirect(list2[:]), rb_all[:], ALU.mult)
-            g_picked.append(picked)
-
-        def front(h):
-            s_picked = sbuf("s_picked%d" % h, [P, J], F32)
-            rounded = sbuf("g_rounded%d" % h, [P, J], BF16)
-            nc.scalar.activation(s_picked[:], s_win[h][:].indirect(list2[:]), COPY)
-            nc.vector.scalar_tensor_tensor(rounded[:], s_picked[:], 0.0, g_picked[h][:], ALU.max, ALU.mult)
-            bank = psum.tile([P, 2, P], F32, name="g_bank%d" % h)
-            turn(bank, rounded)
-            grouped = sbuf("g_grouped%d" % h, [P, P * PACK], BF16)
-            nc.scalar.copy(
-                grouped[:].bitcast(F32).rearrange("p (r u) -> p r u", u=2), bank[:].rearrange("p u r -> p r u")
+        def u_views(c, grouped):
+            return (
+                grouped[:].bitcast(F32).rearrange("p (t r u) -> p t r u", t=2, u=2),
+                u_banks[c][:].rearrange("p t u r -> p t r u"),
             )
-            return grouped
 
-        def back(h, g_mx):
-            g_codes, g_scales = g_mx
-            w_bank = psum.tile([P, PACK, P], F32, name="w_bank%d" % h)
-            for t in range(PACK):
-                nc.tensor.matmul_mx(
-                    out=w_bank[:, t, :],
-                    lhsT=u_codes[:, t * P : (t + 1) * P].bitcast(E4M3),
-                    lhsT_scale=u_scales[:, t * P : (t + 1) * P],
-                    rhs=g_codes[:].bitcast(E5M2),
-                    rhs_scale=g_scales[:],
-                    start=True,
-                    stop=True,
-                )
-            w_grouped = sbuf("w_grouped%d" % h, [P, P * PACK], BF16)
-            nc.scalar.copy(by_four(w_grouped[:]), w_bank[:].rearrange("p t n -> p n t"))
-            w_codes, w_scales = quantise("w%d" % h, w_grouped, P, E5M2)
-            v_bank = psum.tile([P, 2, P], F32, name="v_bank%d" % h, tag="u_bank%d" % h)
-            for r in range(2):
-                nc.tensor.matmul_mx(
-                    out=v_bank[:, r, :],
-                    lhsT=dr_w[:, 2 * P * r : 2 * P * (r + 1)].bitcast(E2M1),
-                    lhsT_scale=dr_s[:, P * r : P * (r + 1)],
-                    rhs=w_codes[:].bitcast(E5M2),
-                    rhs_scale=w_scales[:],
-                    start=True,
-                    stop=True,
-                )
-            result = sbuf("result%d" % h, [P, 2, P], F32)
+        u_grouped0 = placed("u_grouped0", [P, 2 * P * PACK], BF16, 0)
+        nc.vector.tensor_copy(*u_views(0, u_grouped0))
+        u_mx = [quantise("u0", u_grouped0, sbuf("u0_codes", [P, 2 * P], U32), E4M3)]
+
+        s_picked = [placed("s_picked0", [P, J], F32, 20), sbuf("s_picked1", [P, J], F32)]
+        s_part = [stage.tile([P, J], F32, name="s_part%d" % h, offset=6144 + 2048 * h) for h in range(2)]
+        for h in range(2):
+            nc.scalar.activation(s_picked[h][:], s_win[h][:].indirect(list2[:]), COPY)
             nc.vector.scalar_tensor_tensor(
-                result[:], v_bank[:], 0.05, old_part[:, :, h * P : (h + 1) * P], ALU.mult, ALU.max
+                by_four(s_part[h][:]), by_four(s_picked[h][:]), 0.0, rb_all, ALU.max, ALU.mult
             )
-            nc.sync.dma_start(out_rows[:, :, h * P : (h + 1) * P], result[:])
 
-        grouped = [front(h) for h in range(2)]
-        u_codes, u_scales = quantise("u", u_grouped, K, E4M3)
-        g_mx = [quantise("g%d" % h, grouped[h], P, E5M2) for h in range(2)]
-        nc.scalar.activation(old_part[:], old_sb[:], COPY, scale=0.05)
+        g_picked = [placed("g_picked0", [P, J], F32, 30), placed("g_picked1", [P, J], F32, 20)]
+        g_rounded = [sbuf("g_rounded%d" % h, [P, J], BF16) for h in range(2)]
+        share = 3 * J // 8
+        seen["g1"] = g_rounded[1]
+        nc.scalar.activation(g_picked[0][:], g_win[0][:].indirect(list2[:]), COPY)
+        nc.vector.tensor_copy(g_picked[1][:, :share], g_win[1][:].indirect(list2[:, : share // 16]))
+        nc.scalar.activation(g_picked[1][:, share:], g_win[1][:].indirect(list2[:, share // 16 :]), COPY)
+        g_banks = [psum.tile([P, 2, P], F32, name="g_bank%d" % h, tag="g_bank%d" % h) for h in range(2)]
         for h in range(2):
-            back(h, g_mx[h])
+            nc.vector.tensor_tensor(g_rounded[h][:], g_picked[h][:], s_part[h][:], ALU.mult)
+            turn(g_banks[h], g_rounded[h])
+
+        u_grouped1 = placed("u_grouped1", [P, 2 * P * PACK], BF16, 30)
+        nc.scalar.copy(*u_views(1, u_grouped1))
+        u_mx.append(quantise("u1", u_grouped1, placed("u1_codes", [P, 2 * P], U32, 20), E4M3))
+
+        g_mx = []
+        for h in range(2):
+            grouped = placed("g_grouped%d" % h, [P, P * PACK], BF16, 36 + 2 * h)
+            nc.scalar.copy(
+                grouped[:].bitcast(F32).rearrange("p (r u) -> p r u", u=2), g_banks[h][:].rearrange("p u r -> p r u")
+            )
+            g_mx.append(quantise("g%d" % h, grouped, sbuf("g_codes%d" % h, [P, P], U32), E5M2))
+
+        old_part = placed("old_part", [P, 2, N], F32, 38)
+        nc.gpsimd.tensor_scalar(old_part[:], old_sb[:], 0.05, 0.0, ALU.mult, ALU.add)
+        w_tags = (("w_bank0", "w_bank1"), ("ra_bank", "rb_bank"))
+
+        w_mx = []
+        for h in range(2):
+            g_codes, g_scales = g_mx[h]
+            w_grouped = placed("w_grouped%d" % h, [P, P * PACK], BF16, 44 + 2 * h)
+            for c in range(2):
+                u_codes, u_scales = u_mx[c]
+                w_bank = psum.tile([P, 2, P], F32, name="w_bank%d%d" % (h, c), tag=w_tags[h][c])
+                for e in range(2):
+                    nc.tensor.matmul_mx(
+                        out=w_bank[:, e, :],
+                        lhsT=u_codes[:, e * P : (e + 1) * P].bitcast(E4M3),
+                        lhsT_scale=u_scales[:, e * P : (e + 1) * P],
+                        rhs=g_codes[:].bitcast(E5M2),
+                        rhs_scale=g_scales[:],
+                        start=True,
+                        stop=True,
+                    )
+                pair = by_four(w_grouped[:])[:, :, 2 * c : 2 * c + 2]
+                if c == 0:
+                    nc.vector.tensor_copy(pair, w_bank[:].rearrange("p e n -> p n e"))
+                else:
+                    nc.scalar.copy(pair, w_bank[:].rearrange("p e n -> p n e"))
+            w_mx.append(quantise("w%d" % h, w_grouped, sbuf("w_codes%d" % h, [P, P], U32), E5M2))
+
+        def directions(bank, r, h):
+            nc.tensor.matmul_mx(
+                out=bank,
+                lhsT=dr_w[:, 2 * P * r : 2 * P * (r + 1)].bitcast(E2M1),
+                lhsT_scale=dr_s[:, P * r : P * (r + 1)],
+                rhs=w_mx[h][0][:].bitcast(E5M2),
+                rhs_scale=w_mx[h][1][:],
+                start=True,
+                stop=True,
+            )
+
+        v_bank = psum.tile([P, 2, P], F32, name="v_bank0", tag="u_bank0")
+        for r in range(2):
+            directions(v_bank[:, r, :], r, 0)
+        result = placed("result0", [P, 2, P], F32, 46)
+        nc.vector.scalar_tensor_tensor(result[:], v_bank[:], 0.05, old_part[:, :, :P], ALU.mult, ALU.max)
+        nc.sync.dma_start(out.rearrange("(r p) n -> p r n", p=P)[:, :, :P], result[:])
+        for r in range(2):
+            v_last = psum.tile([P, P], F32, name="v_last%d" % r, tag=("u_bank1", "g_bank0")[r])
+            directions(v_last[:], r, 1)
+            last = sbuf("last%d" % r, [P, P], F32)
+            nc.vector.scalar_tensor_tensor(last[:], v_last[:], 0.05, old_part[:, r, P:], ALU.mult, ALU.max)
+            nc.sync.dma_start(out[r * P : (r + 1) * P, P:], last[:])

from contextlib import ExitStack

import concourse.mybir as mybir
from concourse.masks import make_identity

K, J, N, R, T = 512, 512, 256, 256, 1024
FLOPS = 2 * J * K * N + 2 * K * R * N

F32 = mybir.dt.float32
BF16 = mybir.dt.bfloat16
U32 = mybir.dt.uint32
I32 = mybir.dt.int32
U16 = mybir.dt.uint16
U8 = mybir.dt.uint8
E4M3 = mybir.dt.float8_e4m3fn_x4
E5M2 = mybir.dt.float8_e5m2_x4
E2M1 = mybir.dt.float4_e2m1fn_x4
ALU = mybir.AluOpType
COPY = mybir.ActivationFunctionType.Copy

P = 128
PACK = 4


def tile_list_directions_over_saved_larger_kernel(
    tc, xf, ra, lo, gt, rb, sv, fkr, dr_words, dr_scales, old, offs, offs2, out
):
    nc = tc.nc
    with ExitStack() as ctx:
        keep = ctx.enter_context(tc.tile_pool(name="keep", bufs=1))
        stage = ctx.enter_context(tc.tile_pool(name="stage", bufs=1))
        chain = ctx.enter_context(tc.tile_pool(name="chain", bufs=1))
        psum = ctx.enter_context(tc.psum_pool(name="psum", bufs=1))

        def sbuf(name, shape, dtype, tag=""):
            return keep.tile(shape, dtype, name=name, tag=tag or name, align_bytes=64)

        x_rows = xf.rearrange("(p t) v -> p t v", t=PACK)
        x_win = [sbuf("x_win%d" % t, [P, T], F32) for t in range(PACK)]
        g_win = [sbuf("g_win%d" % h, [P, T], F32) for h in range(2)]
        s_win = [sbuf("s_win%d" % h, [P, T], F32) for h in range(2)]
        list1 = keep.tile([P, J // 16], U16, name="list1")
        list2 = keep.tile([P, J // 16], U16, name="list2")
        ra4 = sbuf("ra4", [P, PACK], F32)
        rb4 = sbuf("rb4", [P, PACK], F32)
        lo4 = sbuf("lo4", [P, PACK], F32)
        fk4 = sbuf("fk4", [P, PACK], F32)
        old_sb = sbuf("old_sb", [P, 2, N], F32)
        dr_w = sbuf("dr_w", [P, 2 * R], U8)
        dr_s = sbuf("dr_s", [P, R], U8)
        ident = sbuf("ident", [P, P], F32)

        nc.sync.dma_start(x_win[0][:], x_rows[:, 0, :])
        nc.sync.dma_start(list1[:], offs)
        nc.sync.dma_start(ra4[:], ra.rearrange("o (p t) -> (o p) t", t=PACK))
        nc.sync.dma_start(lo4[:], lo.rearrange("(p t) o -> p (t o)", t=PACK))
        nc.sync.dma_start(fk4[:], fkr.rearrange("o (p t) -> (o p) t", t=PACK))
        nc.sync.dma_start(x_win[1][:], x_rows[:, 1, :])
        nc.sync.dma_start(rb4[:], rb.rearrange("o (p t) -> (o p) t", t=PACK))
        for t in range(2, PACK):
            nc.sync.dma_start(x_win[t][:], x_rows[:, t, :])
        nc.sync.dma_start(list2[:], offs2)
        for h in range(2):
            nc.sync.dma_start(s_win[h][:], sv[h * P : (h + 1) * P, :])
        for h in range(2):
            nc.sync.dma_start(g_win[h][:], gt[h * P : (h + 1) * P, :])
        nc.sync.dma_start(dr_w[:].bitcast(I32), dr_words[0].bitcast(I32))
        nc.sync.dma_start(old_sb[:], old.rearrange("(h p) n -> p h n", p=P))

        ident_narrow = stage.tile([P, 5 * 2 * J], BF16, name="ident_narrow", offset=0)
        make_identity(nc, ident_narrow[:, :P])
        nc.scalar.activation(ident[:], ident_narrow[:, :P], COPY)
        nc.gpsimd.memset(dr_s[:].bitcast(I32), 0)
        for q in range(4):
            nc.sync.dma_start(
                dr_s[32 * q : 32 * q + 4, :].bitcast(I32), dr_scales[0, 4 * q : 4 * q + 4, :].bitcast(I32)
            )

        def placed(name, shape, dtype, half_kib):
            return chain.tile(shape, dtype, name=name, offset=512 * half_kib, align_bytes=64)

        def spread(name, col4):
            bank = psum.tile([P, PACK, P], F32, name=name, tag=name)
            for t in range(PACK):
                nc.tensor.transpose(bank[:, t, :], col4[:, t : t + 1].to_broadcast([P, P]), ident[:])
            return bank[:].rearrange("p t q -> p q t")

        ra_all = spread("ra_bank", ra4)
        rb_all = spread("rb_bank", rb4)

        def by_four(ap):
            return ap.rearrange("p (q t) -> p q t", t=PACK)

        def turn(bank, rounded):
            words = rounded[:].bitcast(F32)
            for u in range(2):
                nc.tensor.transpose(bank[:, u, :], words[:, u : 2 * P : 2], ident[:])

        def quantise(name, grouped, codes, fmt):
            scales = sbuf(name + "_scales", list(codes.shape), U8)
            nc.vector.quantize_mx(out=codes[:].bitcast(fmt), scales=scales[:], in_=grouped[:])
            return codes, scales

        half = J // 2
        seen = {}
        u_banks = [psum.tile([P, 2, 2, P], F32, name="u_bank%d" % c, tag="u_bank%d" % c) for c in range(2)]
        for t in range(PACK):
            picked = stage.tile([P, J], F32, name="x_picked%d" % t, offset=(0, 2048, 4096, 7168)[t])
            if t == 0:
                nc.vector.tensor_copy(picked[:, :half], x_win[t][:].indirect(list1[:, : half // 16]))
                nc.scalar.activation(picked[:, half:], x_win[t][:].indirect(list1[:, half // 16 :]), COPY)
            else:
                nc.scalar.activation(picked[:], x_win[t][:].indirect(list1[:]), COPY)
            over = placed("x_over%d" % t, [P, J], F32, 2 * t)
            nc.vector.tensor_scalar(over[:], picked[:], lo4[:, t : t + 1], 0.0, ALU.subtract, ALU.max)
            rounded = sbuf("u_rounded%d" % t, [P, J], BF16)
            nc.vector.scalar_tensor_tensor(
                by_four(rounded[:]), by_four(over[:]), fk4[:, t : t + 1], ra_all, ALU.mult, ALU.mult
            )
            turn(u_banks[t // 2][:, t % 2], rounded)

        def u_views(c, grouped):
            return (
                grouped[:].bitcast(F32).rearrange("p (t r u) -> p t r u", t=2, u=2),
                u_banks[c][:].rearrange("p t u r -> p t r u"),
            )

        u_grouped0 = placed("u_grouped0", [P, 2 * P * PACK], BF16, 0)
        nc.vector.tensor_copy(*u_views(0, u_grouped0))
        u_mx = [quantise("u0", u_grouped0, sbuf("u0_codes", [P, 2 * P], U32), E4M3)]

        s_picked = [placed("s_picked0", [P, J], F32, 20), sbuf("s_picked1", [P, J], F32)]
        s_part = [stage.tile([P, J], F32, name="s_part%d" % h, offset=6144 + 2048 * h) for h in range(2)]
        for h in range(2):
            nc.scalar.activation(s_picked[h][:], s_win[h][:].indirect(list2[:]), COPY)
            nc.vector.scalar_tensor_tensor(
                by_four(s_part[h][:]), by_four(s_picked[h][:]), 0.0, rb_all, ALU.max, ALU.mult
            )

        g_picked = [placed("g_picked0", [P, J], F32, 30), placed("g_picked1", [P, J], F32, 20)]
        g_rounded = [sbuf("g_rounded%d" % h, [P, J], BF16) for h in range(2)]
        share = 3 * J // 8
        seen["g1"] = g_rounded[1]
        nc.scalar.activation(g_picked[0][:], g_win[0][:].indirect(list2[:]), COPY)
        nc.vector.tensor_copy(g_picked[1][:, :share], g_win[1][:].indirect(list2[:, : share // 16]))
        nc.scalar.activation(g_picked[1][:, share:], g_win[1][:].indirect(list2[:, share // 16 :]), COPY)
        g_banks = [psum.tile([P, 2, P], F32, name="g_bank%d" % h, tag="g_bank%d" % h) for h in range(2)]
        for h in range(2):
            nc.vector.tensor_tensor(g_rounded[h][:], g_picked[h][:], s_part[h][:], ALU.mult)
            turn(g_banks[h], g_rounded[h])

        u_grouped1 = placed("u_grouped1", [P, 2 * P * PACK], BF16, 30)
        nc.scalar.copy(*u_views(1, u_grouped1))
        u_mx.append(quantise("u1", u_grouped1, placed("u1_codes", [P, 2 * P], U32, 20), E4M3))

        g_mx = []
        for h in range(2):
            grouped = placed("g_grouped%d" % h, [P, P * PACK], BF16, 36 + 2 * h)
            nc.scalar.copy(
                grouped[:].bitcast(F32).rearrange("p (r u) -> p r u", u=2), g_banks[h][:].rearrange("p u r -> p r u")
            )
            g_mx.append(quantise("g%d" % h, grouped, sbuf("g_codes%d" % h, [P, P], U32), E5M2))

        old_part = placed("old_part", [P, 2, N], F32, 38)
        nc.gpsimd.tensor_scalar(old_part[:], old_sb[:], 0.05, 0.0, ALU.mult, ALU.add)
        w_tags = (("w_bank0", "w_bank1"), ("ra_bank", "rb_bank"))

        w_mx = []
        for h in range(2):
            g_codes, g_scales = g_mx[h]
            w_grouped = placed("w_grouped%d" % h, [P, P * PACK], BF16, 44 + 2 * h)
            for c in range(2):
                u_codes, u_scales = u_mx[c]
                w_bank = psum.tile([P, 2, P], F32, name="w_bank%d%d" % (h, c), tag=w_tags[h][c])
                for e in range(2):
                    nc.tensor.matmul_mx(
                        out=w_bank[:, e, :],
                        lhsT=u_codes[:, e * P : (e + 1) * P].bitcast(E4M3),
                        lhsT_scale=u_scales[:, e * P : (e + 1) * P],
                        rhs=g_codes[:].bitcast(E5M2),
                        rhs_scale=g_scales[:],
                        start=True,
                        stop=True,
                    )
                pair = by_four(w_grouped[:])[:, :, 2 * c : 2 * c + 2]
                if c == 0:
                    nc.vector.tensor_copy(pair, w_bank[:].rearrange("p e n -> p n e"))
                else:
                    nc.scalar.copy(pair, w_bank[:].rearrange("p e n -> p n e"))
            w_mx.append(quantise("w%d" % h, w_grouped, sbuf("w_codes%d" % h, [P, P], U32), E5M2))

        def directions(bank, r, h):
            nc.tensor.matmul_mx(
                out=bank,
                lhsT=dr_w[:, 2 * P * r : 2 * P * (r + 1)].bitcast(E2M1),
                lhsT_scale=dr_s[:, P * r : P * (r + 1)],
                rhs=w_mx[h][0][:].bitcast(E5M2),
                rhs_scale=w_mx[h][1][:],
                start=True,
                stop=True,
            )

        v_bank = psum.tile([P, 2, P], F32, name="v_bank0", tag="u_bank0")
        for r in range(2):
            directions(v_bank[:, r, :], r, 0)
        result = placed("result0", [P, 2, P], F32, 46)
        nc.vector.scalar_tensor_tensor(result[:], v_bank[:], 0.05, old_part[:, :, :P], ALU.mult, ALU.max)
        nc.sync.dma_start(out.rearrange("(r p) n -> p r n", p=P)[:, :, :P], result[:])
        for r in range(2):
            v_last = psum.tile([P, P], F32, name="v_last%d" % r, tag=("u_bank1", "g_bank0")[r])
            directions(v_last[:], r, 1)
            last = sbuf("last%d" % r, [P, P], F32)
            nc.vector.scalar_tensor_tensor(last[:], v_last[:], 0.05, old_part[:, r, P:], ALU.mult, ALU.max)
            nc.sync.dma_start(out[r * P : (r + 1) * P, P:], last[:])
